import numpy as np
import ml_dtypes


def mxq(x, axis, fmt="e4m3"):
    dtype, down = {"e4m3": (ml_dtypes.float8_e4m3fn, 7), "e5m2": (ml_dtypes.float8_e5m2, 14)}[fmt]
    v = np.moveaxis(np.asarray(x, np.float32).astype(ml_dtypes.bfloat16).astype(np.float64), axis, -1)
    blocks = v.reshape(v.shape[:-1] + (-1, 32))
    amax = np.abs(blocks).max(-1, keepdims=True)
    byte = np.maximum(np.where(amax > 0, np.frexp(amax)[1] - 1 + 127, 0) - down, 1)
    scale = np.exp2(byte - 127.0)
    codes = (blocks / scale).astype(np.float32).astype(dtype).astype(np.float64)
    return np.moveaxis((codes * scale).reshape(v.shape), -1, axis)


WIDE = False


def mx_kscale(k):
    if not WIDE:
        return np.ones(k)
    levels = np.array([10, -10, 5, -5, 0])
    if k % 512:
        return np.exp2(np.random.permutation(np.resize(levels, k // 32))).repeat(32)
    a = np.empty((k // 512, 16))
    for p in range(k // 512):
        a[p, :8] = np.random.permutation(np.resize(levels, 8))
        for g in range(8):
            far = levels[np.abs(levels - a[p, g]) >= 10]
            a[p, g + 8] = far[np.random.randint(len(far))]
    return np.exp2(a.ravel()).repeat(32)


def f64(x):
    return np.asarray(x).astype(np.float64)


def striped(idx):
    return np.tile(np.asarray(idx).reshape(-1, 16).T, (8, 1)).astype(np.uint16)


def unstriped(offs):
    return offs[:16].T.reshape(-1).astype(np.int64)


E2M1 = np.array([0.0, 0.5, 1.0, 1.5, 2.0, 3.0, 4.0, 6.0, -0.0, -0.5, -1.0, -1.5, -2.0, -3.0, -4.0, -6.0])


def pack_weight(w, fmt):
    k, n = w.shape
    w = f64(np.asarray(w, np.float32).astype(ml_dtypes.bfloat16)).reshape(k // 32, 32, n)
    amax = np.abs(w).max(1)
    if fmt == "e4m3":
        byte = np.frexp(amax)[1] - 1 + 127 - 7
    else:
        mant, ex = np.frexp(amax / 6.0)
        byte = np.where(mant > 0.5, ex, ex - 1) + 127
    byte = np.clip(np.where(amax > 0, byte, 1), 1, 254)
    scaled = (w * np.exp2(127.0 - byte)[:, None, :]).reshape(k, n).astype(np.float32)
    by_word = np.ascontiguousarray(scaled.reshape(k // 512, 128, 4, n).transpose(0, 1, 3, 2))
    if fmt == "e4m3":
        words = by_word.astype(ml_dtypes.float8_e4m3fn).view(np.uint8)
    else:
        c = by_word.astype(ml_dtypes.float4_e2m1fn).view(np.uint8) & 0xF
        words = (c[..., 0::2] | (c[..., 1::2] << 4)).reshape(k // 512, 128, 2 * n)
    return np.ascontiguousarray(words), np.ascontiguousarray(byte.astype(np.uint8).reshape(k // 512, 16, n))


def unpack_weight(words, scales, fmt):
    g, _, n = scales.shape
    words = np.ascontiguousarray(words).reshape(g, 128, n, -1)
    if fmt == "e4m3":
        vals = words.view(ml_dtypes.float8_e4m3fn).astype(np.float64)
    else:
        nib = np.empty((g, 128, n, 4), np.uint8)
        nib[..., 0::2] = words & 0xF
        nib[..., 1::2] = words >> 4
        vals = E2M1[nib]
    vals = vals * np.repeat(np.exp2(scales.astype(np.float64) - 127.0), 8, axis=1)[..., None]
    return vals.transpose(0, 1, 3, 2).reshape(g * 512, n)


D, E, T, I, Q = 512, 512, 2048, 512, 128


def setup_inputs():
    n = np.random.standard_normal
    idx2 = np.random.permutation(I)[:I]
    idx = np.random.permutation(T)[:I]
    fd = mx_kscale(D)
    fe = mx_kscale(E)
    keysp = pack_weight(n((D, T)) / fd[:, None], "e2m1")
    valsp = pack_weight(n((E, T)) / fe[:, None], "e2m1")
    return {
        "query": (n((D, Q)) * 0.7 / np.sqrt(D) * fd[:, None]).astype(np.float32),
        "keys_words": keysp[0],
        "keys_scales": keysp[1],
        "gout": (n((E, Q)) * 1 / np.sqrt(E) * fe[:, None]).astype(np.float32),
        "vals_words": valsp[0],
        "vals_scales": valsp[1],
        "old": (0.5 * n((Q, T))).astype(np.float32),
        "offs2": striped(idx2),
        "offs": striped(idx),
    }


def reference(query, keys_words, keys_scales, gout, vals_words, vals_scales, old, offs2, offs):
    idx2 = unstriped(offs2)
    idx = unstriped(offs)
    keysu = unpack_weight(keys_words, keys_scales, "e2m1")
    valsu = unpack_weight(vals_words, vals_scales, "e2m1")
    queryq = mxq(f64(query), 0, "e4m3")
    keysidxg = keysu[:, idx]
    a = queryq.T @ keysidxg
    pa = np.exp(a)
    pb = np.sqrt(pa)
    p = pa * pb[:, idx2]
    z = np.sum(p, axis=1, keepdims=True)
    goutq = mxq(f64(gout), 0, "e4m3")
    valsidxg = valsu[:, idx]
    c0 = goutq.T @ valsidxg
    dz = np.sum(c0 * p / np.square(z) * (-1.0), axis=1, keepdims=True)
    dp = c0 / z + dz
    e1 = dp * pa
    s1 = np.zeros((Q, I))
    s1[:, idx2] = e1
    dpa = dp * pb[:, idx2] + s1 * 0.5 / np.sqrt(pa)
    da = dpa * pa
    gs = da * 512.0
    gf = np.zeros((Q, T))
    gf[:, idx] = gs
    y = f64(old) + gf
    return y

@@ -1,0 +1,141 @@
+import math
+from contextlib import ExitStack
+
+import concourse.mybir as mybir
+
+D, E, T, I, Q = 512, 512, 2048, 512, 128
+FLOPS = 2 * Q * I * (D + E)
+
+F32 = mybir.dt.float32
+BF16 = mybir.dt.bfloat16
+I32 = mybir.dt.int32
+U32 = mybir.dt.uint32
+U16 = mybir.dt.uint16
+U8 = mybir.dt.uint8
+FP8X4 = mybir.dt.float8_e4m3fn_x4
+FP4X4 = mybir.dt.float4_e2m1fn_x4
+ALU = mybir.AluOpType
+ACT = mybir.ActivationFunctionType
+
+P = 128
+PACK = 4
+SOFT = 4.0
+LINK_WINDOW = I + 32
+BACK_WINDOW = 704
+OUT_CHUNKS = (640, 640, 512, 256)
+
+
+def tile_attend_blinkedproduct_s_kernel(tc, query, keys_words, keys_scales, gout, vals_words, vals_scales, old, offs2, offs, out):
+    nc = tc.nc
+    with ExitStack() as ctx:
+        lists = ctx.enter_context(tc.tile_pool(name="lists", bufs=1))
+        sb = ctx.enter_context(tc.tile_pool(name="sb", bufs=1))
+        ps = ctx.enter_context(tc.psum_pool(name="ps", bufs=1))
+
+        tok = lists.tile([P, I // 16], U16, name="tok")
+        link = lists.tile([P, I // 16], U16, name="link")
+
+        k_bytes = sb.tile([P, T], U8, name="k_bytes", align_bytes=64)
+        v_bytes = sb.tile([P, T], U8, name="v_bytes", align_bytes=64)
+        gf = sb.tile([P, T], F32, name="gf")
+        pb = sb.tile([P, LINK_WINDOW], F32, name="pb")
+        warm = sb.tile([P, 1], F32, name="warm")
+        nc.vector.memset(k_bytes[:].bitcast(I32), 0)
+        nc.vector.memset(v_bytes[:].bitcast(I32), 0)
+        nc.vector.memset(warm[:], 0.0)
+        nc.vector.memset(pb[:, I:], 0.0)
+        nc.vector.memset(gf[:], 0.0)
+
+        def load_scales(queue, tile_, src):
+            for quad in range(4):
+                queue.dma_start(out=tile_[32 * quad : 32 * quad + 4, :].bitcast(I32), in_=src[0, 4 * quad : 4 * quad + 4, :].bitcast(I32))
+
+        nc.sync.dma_start(tok[:], offs)
+        load_scales(nc.scalar, k_bytes, keys_scales)
+        q_raw = sb.tile([P, PACK, Q], F32, name="q_raw")
+        nc.sync.dma_start(out=q_raw[:], in_=query.rearrange("(p j) w -> p j w", j=PACK))
+        k_words = sb.tile([P, T], U16, name="k_words", align_bytes=64)
+        nc.sync.dma_start(out=k_words[:].bitcast(I32), in_=keys_words[0].bitcast(I32))
+        g_raw = sb.tile([P, PACK, Q], F32, name="g_raw", tag="gout_then_old")
+        nc.sync.dma_start(out=g_raw[:], in_=gout.rearrange("(p j) w -> p j w", j=PACK))
+        load_scales(nc.sync, v_bytes, vals_scales)
+        v_words = sb.tile([P, T], U16, name="v_words", align_bytes=64)
+        nc.sync.dma_start(out=v_words[:].bitcast(I32), in_=vals_words[0].bitcast(I32))
+        nc.sync.dma_start(link[:], offs2)
+
+        warm_out = sb.tile([P, 1], F32, name="warm_out")
+        nc.scalar.activation(warm_out[:], warm[:], ACT.Exp)
+
+        def interleave(raw, name):
+            grouped = sb.tile([P, Q, PACK], BF16, name=name, align_bytes=64)
+            nc.scalar.copy(grouped[:].rearrange("p (c i) t -> p c t i", i=4), raw[:].rearrange("p t (c i) -> p c t i", i=4))
+            return grouped
+
+        def quantise(grouped, name):
+            codes = sb.tile([P, Q], U32, name=name + "_codes", align_bytes=64)
+            scales = sb.tile([P, Q], U8, name=name + "_scales", align_bytes=64)
+            nc.vector.quantize_mx(out=codes[:].bitcast(FP8X4), scales=scales[:], in_=grouped[:].rearrange("p w j -> p (w j)"))
+            return codes, scales
+
+        def gather(window, dtype, name):
+            picked = sb.tile([P, I], dtype, name=name, align_bytes=64)
+            nc.vector.tensor_copy(picked[:], window[:].indirect(tok[:]))
+            return picked
+
+        def product(codes, scales, words, bytes_, name):
+            acc = ps.tile([P, I], F32, name=name)
+            nc.tensor.matmul_mx(out=acc[:], lhsT=codes[:].bitcast(FP8X4), lhsT_scale=scales[:], rhs=words[:].bitcast(FP4X4), rhs_scale=bytes_[:], start=True, stop=True)
+            return acc
+
+        q_bf = interleave(q_raw, "q_bf")
+        kb = gather(k_bytes, U8, "kb")
+        q_codes, q_scales = quantise(q_bf, "q")
+        kw = gather(k_words, U16, "kw")
+        a = product(q_codes, q_scales, kw, kb, "a")
+
+        g_bf = interleave(g_raw, "g_bf")
+        old_sb = sb.tile([P, T], F32, name="old_sb", tag="gout_then_old")
+        nc.sync.dma_start(out=old_sb[:], in_=old)
+        vb = gather(v_bytes, U8, "vb")
+        g_codes, g_scales = quantise(g_bf, "g")
+        vw = gather(v_words, U16, "vw")
+        c0 = product(g_codes, g_scales, vw, vb, "c0")
+
+        pa = sb.tile([P, I], F32, name="pa")
+        soft_sum = sb.tile([P, 1], F32, name="soft_sum")
+        nc.scalar.activation(pa[:], a[:], ACT.Exp, scale=1.0 / SOFT, accum_out=soft_sum[:])
+        shift = sb.tile([P, 1], F32, name="shift")
+        half_ln2 = 0.5 * SOFT * math.log(2.0)
+        nc.scalar.activation(shift[:], soft_sum[:].bitcast(U32), ACT.Copy, scale=-half_ln2 / 2.0**23, bias=half_ln2 * (127.0 + 0.5 * math.log2(I)))
+        nc.scalar.activation(pb[:, :I], a[:], ACT.Exp, scale=0.5, bias=shift[:])
+        nc.scalar.activation(pa[:], pb[:, :I], ACT.Square)
+
+        p = sb.tile([P, I], F32, name="p")
+        nc.vector.tensor_tensor(p[:], pb[:].indirect(link[:]), pa[:], ALU.mult)
+        z = sb.tile([P, 1], F32, name="z")
+        junk = sb.tile([P, I], F32, name="junk")
+        nc.scalar.activation(junk[:], p[:], ACT.Copy, accum_out=z[:])
+        w = sb.tile([P, I], F32, name="w")
+        s = sb.tile([P, 1], F32, name="s")
+        nc.vector.scalar_tensor_tensor(w[:], c0[:], 1.0, p[:], ALU.mult, ALU.mult, accum_out=s[:])
+        rz = sb.tile([P, 1], F32, name="rz")
+        nc.vector.reciprocal(rz[:], z[:])
+        mu = sb.tile([P, 1], F32, name="mu")
+        nc.vector.tensor_tensor(mu[:], s[:], rz[:], ALU.mult)
+        u = sb.tile([P, I], F32, name="u")
+        nc.vector.scalar_tensor_tensor(u[:], c0[:], mu[:], p[:], ALU.subtract, ALU.mult)
+        back = sb.tile([P, BACK_WINDOW], F32, name="back")
+        nc.vector.tensor_copy(back[:].indirect(link[:]), u[:])
+        u2 = sb.tile([P, I], F32, name="u2")
+        nc.scalar.activation(u2[:], u[:], ACT.Copy, scale=2.0)
+        factor = sb.tile([P, 1], F32, name="factor")
+        nc.scalar.activation(factor[:], rz[:], ACT.Copy, scale=256.0)
+        nc.vector.tensor_tensor(gf[:].indirect(tok[:]), u2[:], back[:, :I], ALU.add)
+
+        start = 0
+        for n, width in enumerate(OUT_CHUNKS):
+            cols = slice(start, start + width)
+            res = sb.tile([P, width], F32, name="res%d" % n)
+            nc.vector.scalar_tensor_tensor(res[:], gf[:, cols], factor[:], old_sb[:, cols], ALU.mult, ALU.add)
+            nc.sync.dma_start(out=out[:, cols], in_=res[:])
+            start += width

@@ -19,10 +19,13 @@ ACT = mybir.ActivationFunctionType
 
 P = 128
 PACK = 4
+BLOCKS = 16
+QUADRANT = 32
+GROUP = 16
+HALF = I // 2
 SOFT = 4.0
-LINK_WINDOW = I + 32
-BACK_WINDOW = 704
-OUT_CHUNKS = (640, 640, 512, 256)
+LINK_WINDOW = 704
+OUT_PIECES = (256, 512, 512, 512, 256)
 
 
 def tile_attend_blinkedproduct_s_kernel(tc, query, keys_words, keys_scales, gout, vals_words, vals_scales, old, offs2, offs, out):
@@ -32,110 +35,124 @@ def tile_attend_blinkedproduct_s_kernel(tc, query, keys_words, keys_scales, gout
         sb = ctx.enter_context(tc.tile_pool(name="sb", bufs=1))
         ps = ctx.enter_context(tc.psum_pool(name="ps", bufs=1))
 
-        tok = lists.tile([P, I // 16], U16, name="tok")
-        link = lists.tile([P, I // 16], U16, name="link")
+        idx = lists.tile([P, I // GROUP], U16, name="idx")
+        idx2 = lists.tile([P, I // GROUP], U16, name="idx2")
+        halves = [(slice(h * HALF, (h + 1) * HALF), slice(h * HALF // GROUP, (h + 1) * HALF // GROUP)) for h in range(2)]
 
-        k_bytes = sb.tile([P, T], U8, name="k_bytes", align_bytes=64)
-        v_bytes = sb.tile([P, T], U8, name="v_bytes", align_bytes=64)
+        key_bytes = sb.tile([P, T], U8, name="key_bytes", align_bytes=64)
+        val_bytes = sb.tile([P, T], U8, name="val_bytes", align_bytes=64)
         gf = sb.tile([P, T], F32, name="gf")
-        pb = sb.tile([P, LINK_WINDOW], F32, name="pb")
-        warm = sb.tile([P, 1], F32, name="warm")
-        nc.vector.memset(k_bytes[:].bitcast(I32), 0)
-        nc.vector.memset(v_bytes[:].bitcast(I32), 0)
-        nc.vector.memset(warm[:], 0.0)
-        nc.vector.memset(pb[:, I:], 0.0)
+        nc.vector.memset(key_bytes[:].bitcast(I32), 0)
+        nc.vector.memset(val_bytes[:].bitcast(I32), 0)
         nc.vector.memset(gf[:], 0.0)
 
-        def load_scales(queue, tile_, src):
-            for quad in range(4):
-                queue.dma_start(out=tile_[32 * quad : 32 * quad + 4, :].bitcast(I32), in_=src[0, 4 * quad : 4 * quad + 4, :].bitcast(I32))
+        def load_words(src, name):
+            words = sb.tile([P, T], U16, name=name, align_bytes=64)
+            nc.sync.dma_start(out=words[:].bitcast(I32), in_=src[0].bitcast(I32))
+            return words
 
-        nc.sync.dma_start(tok[:], offs)
-        load_scales(nc.scalar, k_bytes, keys_scales)
-        q_raw = sb.tile([P, PACK, Q], F32, name="q_raw")
-        nc.sync.dma_start(out=q_raw[:], in_=query.rearrange("(p j) w -> p j w", j=PACK))
-        k_words = sb.tile([P, T], U16, name="k_words", align_bytes=64)
-        nc.sync.dma_start(out=k_words[:].bitcast(I32), in_=keys_words[0].bitcast(I32))
-        g_raw = sb.tile([P, PACK, Q], F32, name="g_raw", tag="gout_then_old")
-        nc.sync.dma_start(out=g_raw[:], in_=gout.rearrange("(p j) w -> p j w", j=PACK))
-        load_scales(nc.sync, v_bytes, vals_scales)
-        v_words = sb.tile([P, T], U16, name="v_words", align_bytes=64)
-        nc.sync.dma_start(out=v_words[:].bitcast(I32), in_=vals_words[0].bitcast(I32))
-        nc.sync.dma_start(link[:], offs2)
+        def load_scale_rows(window, src):
+            for r in range(PACK):
+                nc.sync.dma_start(out=window[r:P:QUADRANT, :].bitcast(I32), in_=src[0, r:BLOCKS:PACK, :].bitcast(I32))
 
-        warm_out = sb.tile([P, 1], F32, name="warm_out")
-        nc.scalar.activation(warm_out[:], warm[:], ACT.Exp)
+        def load_rows(src, name, tag):
+            rows = sb.tile([P, PACK, Q], F32, name=name, tag=tag)
+            nc.sync.dma_start(out=rows[:], in_=src.rearrange("(p t) q -> p t q", t=PACK))
+            return rows
 
-        def interleave(raw, name):
+        key_words = load_words(keys_words, "key_words")
+        nc.sync.dma_start(idx[:], offs)
+        query_rows = load_rows(query, "query_rows", "query_rows")
+        load_scale_rows(key_bytes, keys_scales)
+        val_words = load_words(vals_words, "val_words")
+        load_scale_rows(val_bytes, vals_scales)
+        gout_rows = load_rows(gout, "gout_rows", "gout_then_old")
+        nc.sync.dma_start(idx2[:], offs2)
+
+        def round_and_interleave(copy, rows, name):
             grouped = sb.tile([P, Q, PACK], BF16, name=name, align_bytes=64)
-            nc.scalar.copy(grouped[:].rearrange("p (c i) t -> p c t i", i=4), raw[:].rearrange("p t (c i) -> p c t i", i=4))
+            copy(grouped[:].rearrange("p (c i) t -> p c t i", i=4), rows[:].rearrange("p t (c i) -> p c t i", i=4))
             return grouped
 
         def quantise(grouped, name):
             codes = sb.tile([P, Q], U32, name=name + "_codes", align_bytes=64)
             scales = sb.tile([P, Q], U8, name=name + "_scales", align_bytes=64)
-            nc.vector.quantize_mx(out=codes[:].bitcast(FP8X4), scales=scales[:], in_=grouped[:].rearrange("p w j -> p (w j)"))
+            nc.vector.quantize_mx(out=codes[:].bitcast(FP8X4), scales=scales[:], in_=grouped[:].rearrange("p q t -> p (q t)"))
             return codes, scales
 
-        def gather(window, dtype, name):
-            picked = sb.tile([P, I], dtype, name=name, align_bytes=64)
-            nc.vector.tensor_copy(picked[:], window[:].indirect(tok[:]))
-            return picked
+        def gather_all(window, dtype, name):
+            listed = sb.tile([P, I], dtype, name=name, align_bytes=64)
+            nc.vector.tensor_copy(listed[:], window[:].indirect(idx[:]))
+            return listed
 
-        def product(codes, scales, words, bytes_, name):
-            acc = ps.tile([P, I], F32, name=name)
-            nc.tensor.matmul_mx(out=acc[:], lhsT=codes[:].bitcast(FP8X4), lhsT_scale=scales[:], rhs=words[:].bitcast(FP4X4), rhs_scale=bytes_[:], start=True, stop=True)
-            return acc
+        def product(acc, codes, scales, words, scale_bytes):
+            nc.tensor.matmul_mx(out=acc, lhsT=codes[:].bitcast(FP8X4), lhsT_scale=scales[:], rhs=words.bitcast(FP4X4), rhs_scale=scale_bytes, start=True, stop=True)
 
-        q_bf = interleave(q_raw, "q_bf")
-        kb = gather(k_bytes, U8, "kb")
-        q_codes, q_scales = quantise(q_bf, "q")
-        kw = gather(k_words, U16, "kw")
-        a = product(q_codes, q_scales, kw, kb, "a")
+        query_bf = round_and_interleave(nc.scalar.copy, query_rows, "query_bf")
+        listed_key_words = gather_all(key_words, U16, "listed_key_words")
+        query_codes, query_scales = quantise(query_bf, "query")
+        listed_key_bytes = sb.tile([P, I], U8, name="listed_key_bytes", align_bytes=64)
+        a = ps.tile([P, I], F32, name="a")
+        for slots, entries in halves:
+            nc.vector.tensor_copy(listed_key_bytes[:, slots], key_bytes[:].indirect(idx[:, entries]))
+            product(a[:, slots], query_codes, query_scales, listed_key_words[:, slots], listed_key_bytes[:, slots])
 
-        g_bf = interleave(g_raw, "g_bf")
+        listed_val_words = gather_all(val_words, U16, "listed_val_words")
+        listed_val_bytes = gather_all(val_bytes, U8, "listed_val_bytes")
+        gout_bf = round_and_interleave(nc.vector.tensor_copy, gout_rows, "gout_bf")
+        gout_codes, gout_scales = quantise(gout_bf, "gout")
         old_sb = sb.tile([P, T], F32, name="old_sb", tag="gout_then_old")
         nc.sync.dma_start(out=old_sb[:], in_=old)
-        vb = gather(v_bytes, U8, "vb")
-        g_codes, g_scales = quantise(g_bf, "g")
-        vw = gather(v_words, U16, "vw")
-        c0 = product(g_codes, g_scales, vw, vb, "c0")
+        c0 = ps.tile([P, I], F32, name="c0")
+        product(c0[:], gout_codes, gout_scales, listed_val_words[:], listed_val_bytes[:])
 
-        pa = sb.tile([P, I], F32, name="pa")
+        summed = sb.tile([P, I], F32, name="summed")
         soft_sum = sb.tile([P, 1], F32, name="soft_sum")
-        nc.scalar.activation(pa[:], a[:], ACT.Exp, scale=1.0 / SOFT, accum_out=soft_sum[:])
-        shift = sb.tile([P, 1], F32, name="shift")
-        half_ln2 = 0.5 * SOFT * math.log(2.0)
-        nc.scalar.activation(shift[:], soft_sum[:].bitcast(U32), ACT.Copy, scale=-half_ln2 / 2.0**23, bias=half_ln2 * (127.0 + 0.5 * math.log2(I)))
-        nc.scalar.activation(pb[:, :I], a[:], ACT.Exp, scale=0.5, bias=shift[:])
-        nc.scalar.activation(pa[:], pb[:, :I], ACT.Square)
+        nc.scalar.activation(summed[:], a[:], ACT.Exp, scale=1.0 / SOFT, accum_out=soft_sum[:])
+        per_bit = SOFT * math.log(2.0) / 2.0**23
+        offset = SOFT * math.log(2.0) * (127.0 + 0.5 * math.log2(I))
+        pb_bias = sb.tile([P, 1], F32, name="pb_bias")
+        nc.scalar.activation(pb_bias[:], soft_sum[:].bitcast(U32), ACT.Copy, scale=-0.5 * per_bit, bias=0.5 * offset)
+        pa_bias = sb.tile([P, 1], F32, name="pa_bias")
+        nc.scalar.activation(pa_bias[:], soft_sum[:].bitcast(U32), ACT.Copy, scale=-per_bit, bias=offset)
 
+        pb = sb.tile([P, I], F32, name="pb")
+        nc.scalar.activation(pb[:], a[:], ACT.Exp, scale=0.5, bias=pb_bias[:])
+        pa = sb.tile([P, I], F32, name="pa")
         p = sb.tile([P, I], F32, name="p")
-        nc.vector.tensor_tensor(p[:], pb[:].indirect(link[:]), pa[:], ALU.mult)
+        for slots, entries in halves:
+            nc.scalar.activation(pa[:, slots], a[:, slots], ACT.Exp, bias=pa_bias[:])
+            nc.vector.tensor_tensor(p[:, slots], pb[:].indirect(idx2[:, entries]), pa[:, slots], ALU.mult)
+
+        first, second = halves[0][0], halves[1][0]
+        first_mean = sb.tile([P, 1], F32, name="first_mean")
+        nc.scalar.activation(summed[:, first], p[:, first], ACT.Copy, scale=1.0 / HALF, accum_out=first_mean[:])
         z = sb.tile([P, 1], F32, name="z")
-        junk = sb.tile([P, I], F32, name="junk")
-        nc.scalar.activation(junk[:], p[:], ACT.Copy, accum_out=z[:])
-        w = sb.tile([P, I], F32, name="w")
-        s = sb.tile([P, 1], F32, name="s")
-        nc.vector.scalar_tensor_tensor(w[:], c0[:], 1.0, p[:], ALU.mult, ALU.mult, accum_out=s[:])
+        nc.scalar.activation(summed[:, second], p[:, second], ACT.Identity, bias=first_mean[:], accum_out=z[:])
+
+        weighted = sb.tile([P, I], F32, name="weighted")
+        weighted_sums = [sb.tile([P, 1], F32, name="weighted_sum%d" % h) for h in range(2)]
+        for (slots, entries), total in zip(halves, weighted_sums):
+            nc.vector.scalar_tensor_tensor(weighted[:, slots], c0[:, slots], 1.0, p[:, slots], ALU.mult, ALU.mult, accum_out=total[:])
         rz = sb.tile([P, 1], F32, name="rz")
         nc.vector.reciprocal(rz[:], z[:])
         mu = sb.tile([P, 1], F32, name="mu")
-        nc.vector.tensor_tensor(mu[:], s[:], rz[:], ALU.mult)
+        nc.vector.tensor_scalar(mu[:], weighted_sums[0][:], weighted_sums[1][:], rz[:], ALU.add, ALU.mult)
+
         u = sb.tile([P, I], F32, name="u")
         nc.vector.scalar_tensor_tensor(u[:], c0[:], mu[:], p[:], ALU.subtract, ALU.mult)
-        back = sb.tile([P, BACK_WINDOW], F32, name="back")
-        nc.vector.tensor_copy(back[:].indirect(link[:]), u[:])
-        u2 = sb.tile([P, I], F32, name="u2")
-        nc.scalar.activation(u2[:], u[:], ACT.Copy, scale=2.0)
-        factor = sb.tile([P, 1], F32, name="factor")
-        nc.scalar.activation(factor[:], rz[:], ACT.Copy, scale=256.0)
-        nc.vector.tensor_tensor(gf[:].indirect(tok[:]), u2[:], back[:, :I], ALU.add)
+        linked_u = sb.tile([P, LINK_WINDOW], F32, name="linked_u")
+        nc.vector.tensor_copy(linked_u[:].indirect(idx2[:]), u[:])
+        twice_u = sb.tile([P, I], F32, name="twice_u")
+        nc.scalar.activation(twice_u[:], u[:], ACT.Copy, scale=2.0)
+        row_factor = sb.tile([P, 1], F32, name="row_factor")
+        nc.scalar.activation(row_factor[:], rz[:], ACT.Copy, scale=256.0)
+        nc.vector.tensor_tensor(gf[:].indirect(idx[:]), twice_u[:], linked_u[:, :I], ALU.add)
 
         start = 0
-        for n, width in enumerate(OUT_CHUNKS):
-            cols = slice(start, start + width)
-            res = sb.tile([P, width], F32, name="res%d" % n)
-            nc.vector.scalar_tensor_tensor(res[:], gf[:, cols], factor[:], old_sb[:, cols], ALU.mult, ALU.add)
-            nc.sync.dma_start(out=out[:, cols], in_=res[:])
+        for width in OUT_PIECES:
+            tokens = slice(start, start + width)
+            result = sb.tile([P, width], F32, name="result%d" % start)
+            nc.vector.scalar_tensor_tensor(result[:], gf[:, tokens], row_factor[:], old_sb[:, tokens], ALU.mult, ALU.add)
+            nc.sync.dma_start(out=out[:, tokens], in_=result[:])
             start += width

import math
from contextlib import ExitStack

import concourse.mybir as mybir

D, E, T, I, Q = 512, 512, 2048, 512, 128
FLOPS = 2 * Q * I * (D + E)

F32 = mybir.dt.float32
BF16 = mybir.dt.bfloat16
I32 = mybir.dt.int32
U32 = mybir.dt.uint32
U16 = mybir.dt.uint16
U8 = mybir.dt.uint8
FP8X4 = mybir.dt.float8_e4m3fn_x4
FP4X4 = mybir.dt.float4_e2m1fn_x4
ALU = mybir.AluOpType
ACT = mybir.ActivationFunctionType

P = 128
PACK = 4
BLOCKS = 16
QUADRANT = 32
GROUP = 16
HALF = I // 2
SOFT = 4.0
LINK_WINDOW = 704
OUT_PIECES = (256, 512, 512, 512, 256)


def tile_attend_blinkedproduct_s_kernel(tc, query, keys_words, keys_scales, gout, vals_words, vals_scales, old, offs2, offs, out):
    nc = tc.nc
    with ExitStack() as ctx:
        lists = ctx.enter_context(tc.tile_pool(name="lists", bufs=1))
        sb = ctx.enter_context(tc.tile_pool(name="sb", bufs=1))
        ps = ctx.enter_context(tc.psum_pool(name="ps", bufs=1))

        idx = lists.tile([P, I // GROUP], U16, name="idx")
        idx2 = lists.tile([P, I // GROUP], U16, name="idx2")
        halves = [(slice(h * HALF, (h + 1) * HALF), slice(h * HALF // GROUP, (h + 1) * HALF // GROUP)) for h in range(2)]

        key_bytes = sb.tile([P, T], U8, name="key_bytes", align_bytes=64)
        val_bytes = sb.tile([P, T], U8, name="val_bytes", align_bytes=64)
        gf = sb.tile([P, T], F32, name="gf")
        nc.vector.memset(key_bytes[:].bitcast(I32), 0)
        nc.vector.memset(val_bytes[:].bitcast(I32), 0)
        nc.vector.memset(gf[:], 0.0)

        def load_words(src, name):
            words = sb.tile([P, T], U16, name=name, align_bytes=64)
            nc.sync.dma_start(out=words[:].bitcast(I32), in_=src[0].bitcast(I32))
            return words

        def load_scale_rows(window, src):
            for r in range(PACK):
                nc.sync.dma_start(out=window[r:P:QUADRANT, :].bitcast(I32), in_=src[0, r:BLOCKS:PACK, :].bitcast(I32))

        def load_rows(src, name, tag):
            rows = sb.tile([P, PACK, Q], F32, name=name, tag=tag)
            nc.sync.dma_start(out=rows[:], in_=src.rearrange("(p t) q -> p t q", t=PACK))
            return rows

        key_words = load_words(keys_words, "key_words")
        nc.sync.dma_start(idx[:], offs)
        query_rows = load_rows(query, "query_rows", "query_rows")
        load_scale_rows(key_bytes, keys_scales)
        val_words = load_words(vals_words, "val_words")
        load_scale_rows(val_bytes, vals_scales)
        gout_rows = load_rows(gout, "gout_rows", "gout_then_old")
        nc.sync.dma_start(idx2[:], offs2)

        def round_and_interleave(copy, rows, name):
            grouped = sb.tile([P, Q, PACK], BF16, name=name, align_bytes=64)
            copy(grouped[:].rearrange("p (c i) t -> p c t i", i=4), rows[:].rearrange("p t (c i) -> p c t i", i=4))
            return grouped

        def quantise(grouped, name):
            codes = sb.tile([P, Q], U32, name=name + "_codes", align_bytes=64)
            scales = sb.tile([P, Q], U8, name=name + "_scales", align_bytes=64)
            nc.vector.quantize_mx(out=codes[:].bitcast(FP8X4), scales=scales[:], in_=grouped[:].rearrange("p q t -> p (q t)"))
            return codes, scales

        def gather_all(window, dtype, name):
            listed = sb.tile([P, I], dtype, name=name, align_bytes=64)
            nc.vector.tensor_copy(listed[:], window[:].indirect(idx[:]))
            return listed

        def product(acc, codes, scales, words, scale_bytes):
            nc.tensor.matmul_mx(out=acc, lhsT=codes[:].bitcast(FP8X4), lhsT_scale=scales[:], rhs=words.bitcast(FP4X4), rhs_scale=scale_bytes, start=True, stop=True)

        query_bf = round_and_interleave(nc.scalar.copy, query_rows, "query_bf")
        listed_key_words = gather_all(key_words, U16, "listed_key_words")
        query_codes, query_scales = quantise(query_bf, "query")
        listed_key_bytes = sb.tile([P, I], U8, name="listed_key_bytes", align_bytes=64)
        a = ps.tile([P, I], F32, name="a")
        for slots, entries in halves:
            nc.vector.tensor_copy(listed_key_bytes[:, slots], key_bytes[:].indirect(idx[:, entries]))
            product(a[:, slots], query_codes, query_scales, listed_key_words[:, slots], listed_key_bytes[:, slots])

        listed_val_words = gather_all(val_words, U16, "listed_val_words")
        listed_val_bytes = gather_all(val_bytes, U8, "listed_val_bytes")
        gout_bf = round_and_interleave(nc.vector.tensor_copy, gout_rows, "gout_bf")
        gout_codes, gout_scales = quantise(gout_bf, "gout")
        old_sb = sb.tile([P, T], F32, name="old_sb", tag="gout_then_old")
        nc.sync.dma_start(out=old_sb[:], in_=old)
        c0 = ps.tile([P, I], F32, name="c0")
        product(c0[:], gout_codes, gout_scales, listed_val_words[:], listed_val_bytes[:])

        summed = sb.tile([P, I], F32, name="summed")
        soft_sum = sb.tile([P, 1], F32, name="soft_sum")
        nc.scalar.activation(summed[:], a[:], ACT.Exp, scale=1.0 / SOFT, accum_out=soft_sum[:])
        per_bit = SOFT * math.log(2.0) / 2.0**23
        offset = SOFT * math.log(2.0) * (127.0 + 0.5 * math.log2(I))
        pb_bias = sb.tile([P, 1], F32, name="pb_bias")
        nc.scalar.activation(pb_bias[:], soft_sum[:].bitcast(U32), ACT.Copy, scale=-0.5 * per_bit, bias=0.5 * offset)
        pa_bias = sb.tile([P, 1], F32, name="pa_bias")
        nc.scalar.activation(pa_bias[:], soft_sum[:].bitcast(U32), ACT.Copy, scale=-per_bit, bias=offset)

        pb = sb.tile([P, I], F32, name="pb")
        nc.scalar.activation(pb[:], a[:], ACT.Exp, scale=0.5, bias=pb_bias[:])
        pa = sb.tile([P, I], F32, name="pa")
        p = sb.tile([P, I], F32, name="p")
        for slots, entries in halves:
            nc.scalar.activation(pa[:, slots], a[:, slots], ACT.Exp, bias=pa_bias[:])
            nc.vector.tensor_tensor(p[:, slots], pb[:].indirect(idx2[:, entries]), pa[:, slots], ALU.mult)

        first, second = halves[0][0], halves[1][0]
        first_mean = sb.tile([P, 1], F32, name="first_mean")
        nc.scalar.activation(summed[:, first], p[:, first], ACT.Copy, scale=1.0 / HALF, accum_out=first_mean[:])
        z = sb.tile([P, 1], F32, name="z")
        nc.scalar.activation(summed[:, second], p[:, second], ACT.Identity, bias=first_mean[:], accum_out=z[:])

        weighted = sb.tile([P, I], F32, name="weighted")
        weighted_sums = [sb.tile([P, 1], F32, name="weighted_sum%d" % h) for h in range(2)]
        for (slots, entries), total in zip(halves, weighted_sums):
            nc.vector.scalar_tensor_tensor(weighted[:, slots], c0[:, slots], 1.0, p[:, slots], ALU.mult, ALU.mult, accum_out=total[:])
        rz = sb.tile([P, 1], F32, name="rz")
        nc.vector.reciprocal(rz[:], z[:])
        mu = sb.tile([P, 1], F32, name="mu")
        nc.vector.tensor_scalar(mu[:], weighted_sums[0][:], weighted_sums[1][:], rz[:], ALU.add, ALU.mult)

        u = sb.tile([P, I], F32, name="u")
        nc.vector.scalar_tensor_tensor(u[:], c0[:], mu[:], p[:], ALU.subtract, ALU.mult)
        linked_u = sb.tile([P, LINK_WINDOW], F32, name="linked_u")
        nc.vector.tensor_copy(linked_u[:].indirect(idx2[:]), u[:])
        twice_u = sb.tile([P, I], F32, name="twice_u")
        nc.scalar.activation(twice_u[:], u[:], ACT.Copy, scale=2.0)
        row_factor = sb.tile([P, 1], F32, name="row_factor")
        nc.scalar.activation(row_factor[:], rz[:], ACT.Copy, scale=256.0)
        nc.vector.tensor_tensor(gf[:].indirect(idx[:]), twice_u[:], linked_u[:, :I], ALU.add)

        start = 0
        for width in OUT_PIECES:
            tokens = slice(start, start + width)
            result = sb.tile([P, width], F32, name="result%d" % start)
            nc.vector.scalar_tensor_tensor(result[:], gf[:, tokens], row_factor[:], old_sb[:, tokens], ALU.mult, ALU.add)
            nc.sync.dma_start(out=out[:, tokens], in_=result[:])
            start += width
